import numpy as np
import ml_dtypes


def mxq(x, axis, fmt="e4m3"):
    dtype, down = {"e4m3": (ml_dtypes.float8_e4m3fn, 7), "e5m2": (ml_dtypes.float8_e5m2, 14)}[fmt]
    v = np.moveaxis(np.asarray(x, np.float32).astype(ml_dtypes.bfloat16).astype(np.float64), axis, -1)
    blocks = v.reshape(v.shape[:-1] + (-1, 32))
    amax = np.abs(blocks).max(-1, keepdims=True)
    byte = np.maximum(np.where(amax > 0, np.frexp(amax)[1] - 1 + 127, 0) - down, 1)
    scale = np.exp2(byte - 127.0)
    codes = (blocks / scale).astype(np.float32).astype(dtype).astype(np.float64)
    return np.moveaxis((codes * scale).reshape(v.shape), -1, axis)


WIDE = False


def mx_kscale(k):
    if not WIDE:
        return np.ones(k)
    levels = np.array([30, -30])
    if k % 512:
        return np.exp2(np.random.permutation(np.resize(levels, k // 32))).repeat(32)
    a = np.empty((k // 512, 16))
    for p in range(k // 512):
        a[p, :8] = np.random.permutation(np.resize(levels, 8))
        for g in range(8):
            far = levels[np.abs(levels - a[p, g]) >= 10]
            a[p, g + 8] = far[np.random.randint(len(far))]
    return np.exp2(a.ravel()).repeat(32)


def f64(x):
    return np.asarray(x).astype(np.float64)


def striped(idx):
    return np.tile(np.asarray(idx).reshape(-1, 16).T, (8, 1)).astype(np.uint16)


def unstriped(offs):
    return offs[:16].T.reshape(-1).astype(np.int64)


E2M1 = np.array([0.0, 0.5, 1.0, 1.5, 2.0, 3.0, 4.0, 6.0, -0.0, -0.5, -1.0, -1.5, -2.0, -3.0, -4.0, -6.0])


def pack_weight(w, fmt):
    k, n = w.shape
    w = f64(np.asarray(w, np.float32).astype(ml_dtypes.bfloat16)).reshape(k // 32, 32, n)
    amax = np.abs(w).max(1)
    if fmt in ("e4m3", "e5m2"):
        byte = np.frexp(amax)[1] - 1 + 127 - (7 if fmt == "e4m3" else 14)
    else:
        mant, ex = np.frexp(amax / 6.0)
        byte = np.where(mant > 0.5, ex, ex - 1) + 127
    byte = np.clip(np.where(amax > 0, byte, 1), 1, 254)
    scaled = (w * np.exp2(127.0 - byte)[:, None, :]).reshape(k, n).astype(np.float32)
    by_word = np.ascontiguousarray(scaled.reshape(k // 512, 128, 4, n).transpose(0, 1, 3, 2))
    if fmt in ("e4m3", "e5m2"):
        words = by_word.astype(ml_dtypes.float8_e4m3fn if fmt == "e4m3" else ml_dtypes.float8_e5m2).view(np.uint8)
    else:
        c = by_word.astype(ml_dtypes.float4_e2m1fn).view(np.uint8) & 0xF
        words = (c[..., 0::2] | (c[..., 1::2] << 4)).reshape(k // 512, 128, 2 * n)
    return np.ascontiguousarray(words), np.ascontiguousarray(byte.astype(np.uint8).reshape(k // 512, 16, n))


def unpack_weight(words, scales, fmt):
    g, _, n = scales.shape
    words = np.ascontiguousarray(words).reshape(g, 128, n, -1)
    if fmt in ("e4m3", "e5m2"):
        vals = words.view(ml_dtypes.float8_e4m3fn if fmt == "e4m3" else ml_dtypes.float8_e5m2).astype(np.float64)
    else:
        nib = np.empty((g, 128, n, 4), np.uint8)
        nib[..., 0::2] = words & 0xF
        nib[..., 1::2] = words >> 4
        vals = E2M1[nib]
    vals = vals * np.repeat(np.exp2(scales.astype(np.float64) - 127.0), 8, axis=1)[..., None]
    return vals.transpose(0, 1, 3, 2).reshape(g * 512, n)


def bf(x):
    return np.asarray(x, np.float32).astype(ml_dtypes.bfloat16)


def planes(Y):
    r, m = Y.shape
    b = f64(bf(Y)).reshape(r // 32, 32, m)
    amax = np.abs(b).max(1)
    byte = np.clip(np.where(amax > 0, np.frexp(amax)[1] - 1 + 127 - 7, 1), 1, 254)
    codes = (b * np.exp2(127.0 - byte)[:, None, :]).reshape(r, m).astype(np.float32).astype(ml_dtypes.float8_e4m3fn).view(np.uint8)
    words = codes.reshape(r // 512, 128, 4, m).transpose(0, 1, 3, 2)
    return np.ascontiguousarray(words), np.ascontiguousarray(byte.astype(np.uint8).reshape(r // 512, 16, m))


K, T, J, R, F, N, Z = 512, 512, 256, 512, 512, 512, 512


def setup_inputs():
    n = np.random.standard_normal
    idx = np.random.permutation(T)[:J]
    idx2 = np.random.permutation(Z)[:J]
    fk = mx_kscale(K)
    fr = mx_kscale(R)
    ff = mx_kscale(F)
    wp = pack_weight(n((K, R)) * 1 / np.sqrt(K) * fk[:, None] * fr, "e5m2")
    sxp = pack_weight(n((F, J)) / ff[:, None], "e4m3")
    w2p = pack_weight(n((F, R)) * 1 / np.sqrt(F) * ff[:, None] * fr, "e5m2")
    wbp = pack_weight(n((R, N)) * 1 / np.sqrt(R) / fr[:, None], "e4m3")
    return {
        "xf": (n((K, T))).astype(np.float32),
        "ow": (n((K, J)) * 0.7).astype(np.float32),
        "fk": (np.random.uniform(0.5, 2.0, (K, 1)) / fk[:, None]).astype(np.float32),
        "w_words": wp[0],
        "w_scales": wp[1],
        "sx_words": sxp[0],
        "sx_scales": sxp[1],
        "w2_words": w2p[0],
        "w2_scales": w2p[1],
        "wb_words": wbp[0],
        "wb_scales": wbp[1],
        "tz": (n((N, Z))).astype(np.float32),
        "offs": striped(idx),
        "offs2": striped(idx2),
    }


def reference(xf, ow, fk, w_words, w_scales, sx_words, sx_scales, w2_words, w2_scales, wb_words, wb_scales, tz, offs, offs2):
    idx = unstriped(offs)
    idx2 = unstriped(offs2)
    wu = unpack_weight(w_words, w_scales, "e5m2")
    sxu = unpack_weight(sx_words, sx_scales, "e4m3")
    w2u = unpack_weight(w2_words, w2_scales, "e5m2")
    wbu = unpack_weight(wb_words, wb_scales, "e4m3")
    u = (f64(xf)[:, idx] - f64(ow)) * f64(fk)
    uq = mxq(u, 0, "e5m2")
    a = wu.T @ uq
    q = w2u.T @ sxu
    y1 = np.pad(q, ((0, 0), (1, 0)))[:, :J]
    hid = np.maximum(a, q - 0.6 * y1)
    hidq = mxq(hid, 0, "e5m2")
    p = wbu.T @ hidq
    y = p * f64(tz)[:, idx2]
    words, scales = planes(y)
    return y, words, scales

@@ -1,0 +1,188 @@
+from contextlib import ExitStack
+
+import concourse.mybir as mybir
+
+K, T, J, R, F, N, Z = 512, 512, 256, 512, 512, 512, 512
+FLOPS = 2 * J * (K * R + F * R + R * N)
+
+F32 = mybir.dt.float32
+BF16 = mybir.dt.bfloat16
+I32 = mybir.dt.int32
+U16 = mybir.dt.uint16
+U8 = mybir.dt.uint8
+E4M3 = mybir.dt.float8_e4m3fn_x4
+E5M2 = mybir.dt.float8_e5m2_x4
+ALU = mybir.AluOpType
+COPY = mybir.ActivationFunctionType.Copy
+
+P = 128
+PACK = 4
+HALVES = 2
+JH = J // HALVES
+RUN = 4
+STEP_FACTOR = 0.6
+
+
+def tile_list_two_offsetpicks_own_stepgap_timeslook_pl_kernel(
+    tc, xf, ow, fk, w_words, w_scales, sx_words, sx_scales, w2_words, w2_scales, wb_words, wb_scales, tz, offs, offs2,
+    out_0, out_1, out_2,
+):
+    nc = tc.nc
+    with ExitStack() as ctx:
+        sb = ctx.enter_context(tc.tile_pool(name="sb", bufs=1))
+        psum = ctx.enter_context(tc.psum_pool(name="psum", bufs=1))
+
+        def tile(shape, dtype, name):
+            return sb.tile(shape, dtype, name=name, align_bytes=64)
+
+        def planes(x):
+            return x.rearrange("(p t) c -> p t c", t=PACK)
+
+        def words(x):
+            return x[0].rearrange("p c t -> p (c t)").bitcast(I32)
+
+        def half(h):
+            return slice(h * JH, (h + 1) * JH)
+
+        offsets = sb.tile([P, J // 16], U16, name="offsets")
+        offsets2 = sb.tile([P, J // 16], U16, name="offsets2")
+        xf_sb = [tile([P, T], F32, f"xf{t}") for t in range(PACK)]
+        tz_sb = [tile([P, Z], F32, f"tz{t}") for t in range(PACK)]
+        ow_sb = [tile([P, 2, J], F32, f"ow{h}") for h in range(2)]
+        fk_sb = tile([P, PACK], F32, "fk_sb")
+        raw = [tile([P, R], I32, f"raw{i}") for i in range(3)]
+        dealt = [tile([P, R], I32, f"dealt{i}") for i in range(3)]
+        sx_sb = tile([P, J], I32, "sx_sb")
+        raw_scales = tile([P, 3 * R], U8, "raw_scales")
+        scales = tile([P, 3 * R + J], U8, "scales")
+        W2, W, WB = 0, 1, 2
+
+        nc.vector.memset(raw_scales[:].bitcast(I32), 0)
+        nc.vector.memset(scales[:, 3 * R :].bitcast(I32), 0)
+        for i, src in ((W2, w2_scales), (W, w_scales), (WB, wb_scales)):
+            nc.scalar.dma_start(raw_scales[0:16, i * R : (i + 1) * R].bitcast(I32), src[0].bitcast(I32))
+        nc.scalar.dma_start(scales[0:16, 3 * R :].bitcast(I32), sx_scales[0].bitcast(I32))
+        nc.scalar.dma_start(fk_sb[:], fk.rearrange("(p t) o -> p (t o)", t=PACK))
+
+        nc.sync.dma_start(offsets[:], offs)
+        nc.sync.dma_start(xf_sb[0][:], planes(xf)[:, 0, :])
+        nc.sync.dma_start(xf_sb[1][:], planes(xf)[:, 1, :])
+        nc.sync.dma_start(ow_sb[0][:], planes(ow)[:, 0:2, :])
+        nc.sync.dma_start(raw[W2][:], words(w2_words))
+        nc.sync.dma_start(sx_sb[:], words(sx_words))
+        nc.sync.dma_start(xf_sb[2][:], planes(xf)[:, 2, :])
+        nc.sync.dma_start(xf_sb[3][:], planes(xf)[:, 3, :])
+        nc.sync.dma_start(ow_sb[1][:], planes(ow)[:, 2:4, :])
+        nc.sync.dma_start(raw[W][:], words(w_words))
+        nc.sync.dma_start(raw[WB][:], words(wb_words))
+        nc.sync.dma_start(offsets2[:], offs2)
+        for t in range(PACK):
+            nc.sync.dma_start(tz_sb[t][:], planes(tz)[:, t, :])
+
+        nc.vector.tensor_copy(
+            scales[:, 0 : 3 * R].rearrange("p (w t m) -> p w t m", w=3, t=PACK),
+            raw_scales[:].rearrange("p (w m t) -> p w t m", w=3, t=PACK),
+        )
+        for q in range(1, 4):
+            nc.scalar.dma_start(scales[32 * q : 32 * q + 4, :].bitcast(I32), scales[4 * q : 4 * q + 4, :].bitcast(I32))
+
+        def deal(i):
+            nc.vector.tensor_copy(
+                dealt[i][:].rearrange("p (t c i) -> p c t i", t=PACK, i=RUN),
+                raw[i][:].rearrange("p (c i t) -> p c t i", t=PACK, i=RUN),
+            )
+
+        def product(acc, i, fmt, rhs, rhs_scale):
+            for t in range(PACK):
+                nc.tensor.matmul_mx(
+                    out=acc[:, t, :],
+                    lhsT=dealt[i][:, t * P : (t + 1) * P].bitcast(fmt),
+                    lhsT_scale=scales[:, i * R + t * P : i * R + (t + 1) * P],
+                    rhs=rhs,
+                    rhs_scale=rhs_scale,
+                    start=True,
+                    stop=True,
+                )
+
+        def woven(x):
+            return x.rearrange("p (c i t) -> p c t i", t=PACK, i=RUN)
+
+        def by_plane(x):
+            return x.rearrange("p t (c i) -> p c t i", i=RUN)
+
+        xg = tile([P, PACK, J], F32, "xg")
+        diff = tile([P, PACK, J], F32, "diff")
+
+        def centre(t):
+            nc.scalar.activation(xg[:, t, :], xf_sb[t][:].indirect(offsets[:]), COPY)
+            nc.vector.tensor_tensor(diff[:, t, :], xg[:, t, :], ow_sb[t // 2][:, t % 2, :], ALU.subtract)
+
+        centre(0)
+        centre(1)
+
+        deal(W2)
+        q_sb = tile([P, (J + 1) * PACK], F32, "q_sb")
+        step = tile([P, J * PACK], F32, "step")
+        nc.vector.memset(q_sb[:, 0:PACK], 0.0)
+        for h in range(HALVES):
+            q_ps = psum.tile([P, PACK, JH], F32, name=f"q_ps{h}")
+            product(q_ps, W2, E5M2, sx_sb[:, half(h)].bitcast(E4M3), scales[:, 3 * R + h * JH : 3 * R + (h + 1) * JH])
+            lo, hi = h * JH * PACK, (h + 1) * JH * PACK
+            nc.scalar.activation(
+                q_sb[:, lo + PACK : hi + PACK].rearrange("p (j t) -> p j t", t=PACK),
+                q_ps[:].rearrange("p t j -> p j t"),
+                COPY,
+            )
+            nc.vector.scalar_tensor_tensor(
+                step[:, lo:hi], q_sb[:, lo:hi], -STEP_FACTOR, q_sb[:, lo + PACK : hi + PACK], ALU.mult, ALU.add
+            )
+
+        centre(2)
+        centre(3)
+        deal(W)
+        factor = fk_sb[:].unsqueeze(1).unsqueeze(3).to_broadcast([P, JH // RUN, PACK, RUN])
+        u_bf = [tile([P, JH * PACK], BF16, f"u_bf{h}") for h in range(HALVES)]
+        u_codes = [tile([P, JH], I32, f"u_codes{h}") for h in range(HALVES)]
+        u_scales = [tile([P, JH], U8, f"u_scales{h}") for h in range(HALVES)]
+        for h in range(HALVES):
+            nc.vector.tensor_tensor(woven(u_bf[h][:]), by_plane(diff[:, :, half(h)]), factor, ALU.mult)
+        a_ps = [psum.tile([P, PACK, JH], F32, name=f"a_ps{h}") for h in range(HALVES)]
+        for h in range(HALVES):
+            nc.vector.quantize_mx(out=u_codes[h][:].bitcast(E5M2), scales=u_scales[h][:], in_=u_bf[h][:])
+            product(a_ps[h], W, E5M2, u_codes[h][:].bitcast(E5M2), u_scales[h][:])
+        deal(WB)
+
+        hid_bf = [tile([P, JH * PACK], BF16, f"hid_bf{h}") for h in range(HALVES)]
+        hid_codes = [tile([P, JH], I32, f"hid_codes{h}") for h in range(HALVES)]
+        hid_scales = [tile([P, JH], U8, f"hid_scales{h}") for h in range(HALVES)]
+        for h in range(HALVES):
+            nc.vector.tensor_tensor(
+                hid_bf[h][:].rearrange("p (j t) -> p j t", t=PACK),
+                a_ps[h][:].rearrange("p t j -> p j t"),
+                step[:, h * JH * PACK : (h + 1) * JH * PACK].rearrange("p (j t) -> p j t", t=PACK),
+                ALU.max,
+            )
+        p_ps = [psum.tile([P, PACK, JH], F32, name=f"p_ps{h}") for h in range(HALVES)]
+        for h in range(HALVES):
+            nc.vector.quantize_mx(out=hid_codes[h][:].bitcast(E5M2), scales=hid_scales[h][:], in_=hid_bf[h][:])
+            product(p_ps[h], WB, E4M3, hid_codes[h][:].bitcast(E5M2), hid_scales[h][:])
+
+        tzg = tile([P, PACK, J], F32, "tzg")
+        for t in range(PACK):
+            nc.scalar.activation(tzg[:, t, :], tz_sb[t][:].indirect(offsets2[:]), COPY)
+
+        y = [tile([P, PACK, JH], F32, f"y{h}") for h in range(HALVES)]
+        y_bf = [tile([P, JH * PACK], BF16, f"y_bf{h}") for h in range(HALVES)]
+        y_codes = tile([P, J], I32, "y_codes")
+        y_scales = tile([P, J], U8, "y_scales")
+        for h in range(HALVES):
+            nc.vector.tensor_tensor(y[h][:], p_ps[h][:], tzg[:, :, half(h)], ALU.mult)
+            nc.sync.dma_start(planes(out_0)[:, :, half(h)], y[h][:])
+        nc.scalar.activation(woven(y_bf[0][:]), by_plane(y[0][:]), COPY)
+        nc.vector.tensor_copy(woven(y_bf[1][:]), by_plane(y[1][:]))
+        for h in range(HALVES):
+            nc.vector.quantize_mx(out=y_codes[:, half(h)].bitcast(E4M3), scales=y_scales[:, half(h)], in_=y_bf[h][:])
+        nc.sync.dma_start(words(out_1), y_codes[:])
+        for q in range(4):
+            eng = nc.scalar if q % 2 == 0 else nc.sync
+            eng.dma_start(out_2[0, 4 * q : 4 * q + 4, :].bitcast(I32), y_scales[32 * q : 32 * q + 4, :].bitcast(I32))

@@ -30,6 +30,7 @@ def tile_list_two_offsetpicks_own_stepgap_timeslook_pl_kernel(
     nc = tc.nc
     with ExitStack() as ctx:
         sb = ctx.enter_context(tc.tile_pool(name="sb", bufs=1))
+        staging = ctx.enter_context(tc.tile_pool(name="staging", bufs=1))
         psum = ctx.enter_context(tc.psum_pool(name="psum", bufs=1))
 
         def tile(shape, dtype, name):
@@ -46,45 +47,54 @@ def tile_list_two_offsetpicks_own_stepgap_timeslook_pl_kernel(
 
         offsets = sb.tile([P, J // 16], U16, name="offsets")
         offsets2 = sb.tile([P, J // 16], U16, name="offsets2")
-        xf_sb = [tile([P, T], F32, f"xf{t}") for t in range(PACK)]
-        tz_sb = [tile([P, Z], F32, f"tz{t}") for t in range(PACK)]
-        ow_sb = [tile([P, 2, J], F32, f"ow{h}") for h in range(2)]
+        def shared(shape, dtype, name, tag):
+            return sb.tile(shape, dtype, name=name, tag=tag, align_bytes=64)
+
+        xf_a = shared([P, 2, T], F32, "xf_a", "table_a")
+        xf_b = shared([P, T], F32, "xf_b", "table_b")
+        xf_c = shared([P, T], F32, "xf_c", "table_c")
+        ow_sb = tile([P, PACK, J], F32, "ow_sb")
         fk_sb = tile([P, PACK], F32, "fk_sb")
-        raw = [tile([P, R], I32, f"raw{i}") for i in range(3)]
-        dealt = [tile([P, R], I32, f"dealt{i}") for i in range(3)]
-        sx_sb = tile([P, J], I32, "sx_sb")
-        raw_scales = tile([P, 3 * R], U8, "raw_scales")
-        scales = tile([P, 3 * R + J], U8, "scales")
         W2, W, WB = 0, 1, 2
+        raw_scales = staging.tile([P, 3 * R], U8, name="raw_scales", offset=4 * R - 3 * R // 2, align_bytes=64)
+        raw_w2 = tile([P, R], I32, "raw_w2")
+        dealt = [shared([P, R], I32, "dealt_w2", "picked"), tile([P, R], I32, "dealt_w"), tile([P, R], I32, "dealt_wb")]
+        sx_sb = tile([P, J], I32, "sx_sb")
+        scales = tile([P, 3 * R + J], U8, "scales")
 
-        nc.vector.memset(raw_scales[:].bitcast(I32), 0)
-        nc.vector.memset(scales[:, 3 * R :].bitcast(I32), 0)
+        def load_scales(dst, src):
+            nc.sync.dma_start(dst.bitcast(I32), src[0].bitcast(I32).partition_broadcast(P // 16))
+
+        q_sb = tile([P, (J + 1) * PACK], F32, "q_sb")
+        zero = tile([P, PACK], F32, "zero")
+        nc.vector.memset(zero[:], 0.0)
+        nc.scalar.activation(q_sb[:, 0:PACK], zero[:], COPY)
+
         for i, src in ((W2, w2_scales), (W, w_scales), (WB, wb_scales)):
-            nc.scalar.dma_start(raw_scales[0:16, i * R : (i + 1) * R].bitcast(I32), src[0].bitcast(I32))
-        nc.scalar.dma_start(scales[0:16, 3 * R :].bitcast(I32), sx_scales[0].bitcast(I32))
-        nc.scalar.dma_start(fk_sb[:], fk.rearrange("(p t) o -> p (t o)", t=PACK))
-
+            load_scales(raw_scales[:, i * R : (i + 1) * R], src)
+        load_scales(scales[:, 3 * R :], sx_scales)
         nc.sync.dma_start(offsets[:], offs)
-        nc.sync.dma_start(xf_sb[0][:], planes(xf)[:, 0, :])
-        nc.sync.dma_start(xf_sb[1][:], planes(xf)[:, 1, :])
-        nc.sync.dma_start(ow_sb[0][:], planes(ow)[:, 0:2, :])
-        nc.sync.dma_start(raw[W2][:], words(w2_words))
-        nc.sync.dma_start(sx_sb[:], words(sx_words))
-        nc.sync.dma_start(xf_sb[2][:], planes(xf)[:, 2, :])
-        nc.sync.dma_start(xf_sb[3][:], planes(xf)[:, 3, :])
-        nc.sync.dma_start(ow_sb[1][:], planes(ow)[:, 2:4, :])
-        nc.sync.dma_start(raw[W][:], words(w_words))
-        nc.sync.dma_start(raw[WB][:], words(wb_words))
+        nc.sync.dma_start(xf_a[:], planes(xf)[:, 0:2, :])
+        nc.sync.dma_start(fk_sb[:], fk.rearrange("(p t) o -> p (t o)", t=PACK))
+        nc.sync.dma_start(ow_sb[:], planes(ow))
         nc.sync.dma_start(offsets2[:], offs2)
-        for t in range(PACK):
-            nc.sync.dma_start(tz_sb[t][:], planes(tz)[:, t, :])
+        nc.sync.dma_start(xf_b[:], planes(xf)[:, 2, :])
+        nc.sync.dma_start(xf_c[:], planes(xf)[:, 3, :])
+        nc.sync.dma_start(raw_w2[:], words(w2_words))
+        nc.sync.dma_start(sx_sb[:], words(sx_words))
 
         nc.vector.tensor_copy(
-            scales[:, 0 : 3 * R].rearrange("p (w t m) -> p w t m", w=3, t=PACK),
-            raw_scales[:].rearrange("p (w m t) -> p w t m", w=3, t=PACK),
+            scales[:, 0 : 3 * R].rearrange("p (w t m) -> p t w m", w=3, t=PACK),
+            raw_scales[:].rearrange("p (w m t) -> p t w m", w=3, t=PACK),
         )
         for q in range(1, 4):
-            nc.scalar.dma_start(scales[32 * q : 32 * q + 4, :].bitcast(I32), scales[4 * q : 4 * q + 4, :].bitcast(I32))
+            nc.sync.dma_start(scales[32 * q : 32 * q + 4, :].bitcast(I32), scales[4 * q : 4 * q + 4, :].bitcast(I32))
+
+        raw_w = staging.tile([P, R], I32, name="raw_w", offset=0, align_bytes=64)
+        raw_wb = staging.tile([P, R], I32, name="raw_wb", offset=4 * R, align_bytes=64)
+        raw = [raw_w2, raw_w, raw_wb]
+        nc.sync.dma_start(raw_w[:], words(w_words))
+        nc.sync.dma_start(raw_wb[:], words(wb_words))
 
         def deal(i):
             nc.vector.tensor_copy(
@@ -110,66 +120,88 @@ def tile_list_two_offsetpicks_own_stepgap_timeslook_pl_kernel(
         def by_plane(x):
             return x.rearrange("p t (c i) -> p c t i", i=RUN)
 
-        xg = tile([P, PACK, J], F32, "xg")
+        xg = tile([P, 2, J], F32, "xg")
         diff = tile([P, PACK, J], F32, "diff")
+        u_pl = tile([P, PACK, J], BF16, "u_pl")
 
-        def centre(t):
-            nc.scalar.activation(xg[:, t, :], xf_sb[t][:].indirect(offsets[:]), COPY)
-            nc.vector.tensor_tensor(diff[:, t, :], xg[:, t, :], ow_sb[t // 2][:, t % 2, :], ALU.subtract)
+        def scale(t):
+            nc.scalar.activation(u_pl[:, t, :], diff[:, t, :], COPY, scale=fk_sb[:, t : t + 1])
 
-        centre(0)
-        centre(1)
+        for t in range(2):
+            nc.scalar.activation(xg[:, t, :], xf_a[:, t, :].indirect(offsets[:]), COPY)
+        nc.vector.tensor_tensor(diff[:, 0:2, :], xg[:], ow_sb[:, 0:2, :], ALU.subtract)
+        for t in range(2):
+            scale(t)
+        for t, win in ((2, xf_b), (3, xf_c)):
+            nc.vector.tensor_tensor(diff[:, t, :], win[:].indirect(offsets[:]), ow_sb[:, t, :], ALU.subtract)
+            scale(t)
+
+        tz_a = shared([P, 2, Z], F32, "tz_a", "table_a")
+        tz_b = shared([P, Z], F32, "tz_b", "table_b")
+        tz_c = shared([P, Z], F32, "tz_c", "table_c")
+        tz_win = [tz_a[:, 0, :], tz_a[:, 1, :], tz_b[:], tz_c[:]]
+        nc.sync.dma_start(tz_a[:], planes(tz)[:, 0:2, :])
+        nc.sync.dma_start(tz_b[:], planes(tz)[:, 2, :])
+        nc.sync.dma_start(tz_c[:], planes(tz)[:, 3, :])
 
         deal(W2)
-        q_sb = tile([P, (J + 1) * PACK], F32, "q_sb")
-        step = tile([P, J * PACK], F32, "step")
-        nc.vector.memset(q_sb[:, 0:PACK], 0.0)
+        q_ps = [psum.tile([P, PACK, JH], F32, name=f"q_ps{h}") for h in range(HALVES)]
         for h in range(HALVES):
-            q_ps = psum.tile([P, PACK, JH], F32, name=f"q_ps{h}")
-            product(q_ps, W2, E5M2, sx_sb[:, half(h)].bitcast(E4M3), scales[:, 3 * R + h * JH : 3 * R + (h + 1) * JH])
+            product(q_ps[h], W2, E5M2, sx_sb[:, half(h)].bitcast(E4M3), scales[:, 3 * R + h * JH : 3 * R + (h + 1) * JH])
+
+        u_bf = [tile([P, JH * PACK], BF16, f"u_bf{h}") for h in range(HALVES)]
+        u_codes = [tile([P, JH], I32, f"u_codes{h}") for h in range(HALVES)]
+        u_scales = [tile([P, JH], U8, f"u_scales{h}") for h in range(HALVES)]
+        deal(W)
+        nc.vector.tensor_copy(woven(u_bf[0][:]), by_plane(u_pl[:, :, half(0)]))
+        nc.scalar.copy(woven(u_bf[1][:]), by_plane(u_pl[:, :, half(1)]))
+        deal(WB)
+        a_ps = [psum.tile([P, PACK, JH], F32, name=f"a_ps{h}") for h in range(HALVES)]
+        p_ps = [psum.tile([P, PACK, JH], F32, name=f"p_ps{h}") for h in range(HALVES)]
+        step = tile([P, J * PACK], F32, "step")
+        hid_bf = [tile([P, JH * PACK], BF16, f"hid_bf{h}") for h in range(HALVES)]
+        hid_codes = [tile([P, JH], I32, f"hid_codes{h}") for h in range(HALVES)]
+        hid_scales = [tile([P, JH], U8, f"hid_scales{h}") for h in range(HALVES)]
+
+        def first(h):
+            nc.vector.quantize_mx(out=u_codes[h][:].bitcast(E5M2), scales=u_scales[h][:], in_=u_bf[h][:])
+            product(a_ps[h], W, E5M2, u_codes[h][:].bitcast(E5M2), u_scales[h][:])
+
+        def stepped(h):
             lo, hi = h * JH * PACK, (h + 1) * JH * PACK
             nc.scalar.activation(
                 q_sb[:, lo + PACK : hi + PACK].rearrange("p (j t) -> p j t", t=PACK),
-                q_ps[:].rearrange("p t j -> p j t"),
+                q_ps[h][:].rearrange("p t j -> p j t"),
                 COPY,
             )
             nc.vector.scalar_tensor_tensor(
                 step[:, lo:hi], q_sb[:, lo:hi], -STEP_FACTOR, q_sb[:, lo + PACK : hi + PACK], ALU.mult, ALU.add
             )
 
-        centre(2)
-        centre(3)
-        deal(W)
-        factor = fk_sb[:].unsqueeze(1).unsqueeze(3).to_broadcast([P, JH // RUN, PACK, RUN])
-        u_bf = [tile([P, JH * PACK], BF16, f"u_bf{h}") for h in range(HALVES)]
-        u_codes = [tile([P, JH], I32, f"u_codes{h}") for h in range(HALVES)]
-        u_scales = [tile([P, JH], U8, f"u_scales{h}") for h in range(HALVES)]
-        for h in range(HALVES):
-            nc.vector.tensor_tensor(woven(u_bf[h][:]), by_plane(diff[:, :, half(h)]), factor, ALU.mult)
-        a_ps = [psum.tile([P, PACK, JH], F32, name=f"a_ps{h}") for h in range(HALVES)]
-        for h in range(HALVES):
-            nc.vector.quantize_mx(out=u_codes[h][:].bitcast(E5M2), scales=u_scales[h][:], in_=u_bf[h][:])
-            product(a_ps[h], W, E5M2, u_codes[h][:].bitcast(E5M2), u_scales[h][:])
-        deal(WB)
-
-        hid_bf = [tile([P, JH * PACK], BF16, f"hid_bf{h}") for h in range(HALVES)]
-        hid_codes = [tile([P, JH], I32, f"hid_codes{h}") for h in range(HALVES)]
-        hid_scales = [tile([P, JH], U8, f"hid_scales{h}") for h in range(HALVES)]
-        for h in range(HALVES):
+        def hidden(h):
             nc.vector.tensor_tensor(
                 hid_bf[h][:].rearrange("p (j t) -> p j t", t=PACK),
                 a_ps[h][:].rearrange("p t j -> p j t"),
                 step[:, h * JH * PACK : (h + 1) * JH * PACK].rearrange("p (j t) -> p j t", t=PACK),
                 ALU.max,
             )
-        p_ps = [psum.tile([P, PACK, JH], F32, name=f"p_ps{h}") for h in range(HALVES)]
-        for h in range(HALVES):
+
+        def second(h):
             nc.vector.quantize_mx(out=hid_codes[h][:].bitcast(E5M2), scales=hid_scales[h][:], in_=hid_bf[h][:])
             product(p_ps[h], WB, E4M3, hid_codes[h][:].bitcast(E5M2), hid_scales[h][:])
 
-        tzg = tile([P, PACK, J], F32, "tzg")
+        first(0)
+        stepped(0)
+        first(1)
+        hidden(0)
+        stepped(1)
+        second(0)
+        hidden(1)
+        second(1)
+
+        tzg = shared([P, PACK, J], F32, "tzg", "picked")
         for t in range(PACK):
-            nc.scalar.activation(tzg[:, t, :], tz_sb[t][:].indirect(offsets2[:]), COPY)
+            nc.scalar.activation(tzg[:, t, :], tz_win[t].indirect(offsets2[:]), COPY)
 
         y = [tile([P, PACK, JH], F32, f"y{h}") for h in range(HALVES)]
         y_bf = [tile([P, JH * PACK], BF16, f"y_bf{h}") for h in range(HALVES)]

@@ -58,7 +58,7 @@ def tile_list_two_offsetpicks_own_stepgap_timeslook_pl_kernel(
         W2, W, WB = 0, 1, 2
         raw_scales = staging.tile([P, 3 * R], U8, name="raw_scales", offset=4 * R - 3 * R // 2, align_bytes=64)
         raw_w2 = tile([P, R], I32, "raw_w2")
-        dealt = [shared([P, R], I32, "dealt_w2", "picked"), tile([P, R], I32, "dealt_w"), tile([P, R], I32, "dealt_wb")]
+        dealt = [shared([P, R], I32, "dealt_w2", "picked"), tile([P, R], I32, "dealt_w"), None]
         sx_sb = tile([P, J], I32, "sx_sb")
         scales = tile([P, 3 * R + J], U8, "scales")
 
@@ -122,15 +122,15 @@ def tile_list_two_offsetpicks_own_stepgap_timeslook_pl_kernel(
 
         xg = tile([P, 2, J], F32, "xg")
         diff = tile([P, PACK, J], F32, "diff")
-        u_pl = tile([P, PACK, J], BF16, "u_pl")
+        u_pl = shared([P, PACK, J], BF16, "u_pl", "late_weight")
 
         def scale(t):
             nc.scalar.activation(u_pl[:, t, :], diff[:, t, :], COPY, scale=fk_sb[:, t : t + 1])
 
         for t in range(2):
             nc.scalar.activation(xg[:, t, :], xf_a[:, t, :].indirect(offsets[:]), COPY)
-        nc.vector.tensor_tensor(diff[:, 0:2, :], xg[:], ow_sb[:, 0:2, :], ALU.subtract)
         for t in range(2):
+            nc.vector.tensor_tensor(diff[:, t, :], xg[:, t, :], ow_sb[:, t, :], ALU.subtract)
             scale(t)
         for t, win in ((2, xf_b), (3, xf_c)):
             nc.vector.tensor_tensor(diff[:, t, :], win[:].indirect(offsets[:]), ow_sb[:, t, :], ALU.subtract)
@@ -152,10 +152,9 @@ def tile_list_two_offsetpicks_own_stepgap_timeslook_pl_kernel(
         u_bf = [tile([P, JH * PACK], BF16, f"u_bf{h}") for h in range(HALVES)]
         u_codes = [tile([P, JH], I32, f"u_codes{h}") for h in range(HALVES)]
         u_scales = [tile([P, JH], U8, f"u_scales{h}") for h in range(HALVES)]
-        deal(W)
         nc.vector.tensor_copy(woven(u_bf[0][:]), by_plane(u_pl[:, :, half(0)]))
         nc.scalar.copy(woven(u_bf[1][:]), by_plane(u_pl[:, :, half(1)]))
-        deal(WB)
+        deal(W)
         a_ps = [psum.tile([P, PACK, JH], F32, name=f"a_ps{h}") for h in range(HALVES)]
         p_ps = [psum.tile([P, PACK, JH], F32, name=f"p_ps{h}") for h in range(HALVES)]
         step = tile([P, J * PACK], F32, "step")
@@ -191,6 +190,8 @@ def tile_list_two_offsetpicks_own_stepgap_timeslook_pl_kernel(
             product(p_ps[h], WB, E4M3, hid_codes[h][:].bitcast(E5M2), hid_scales[h][:])
 
         first(0)
+        dealt[WB] = shared([P, R], I32, "dealt_wb", "late_weight")
+        deal(WB)
         stepped(0)
         first(1)
         hidden(0)
@@ -214,7 +215,7 @@ def tile_list_two_offsetpicks_own_stepgap_timeslook_pl_kernel(
         nc.vector.tensor_copy(woven(y_bf[1][:]), by_plane(y[1][:]))
         for h in range(HALVES):
             nc.vector.quantize_mx(out=y_codes[:, half(h)].bitcast(E4M3), scales=y_scales[:, half(h)], in_=y_bf[h][:])
-        nc.sync.dma_start(words(out_1), y_codes[:])
+            nc.sync.dma_start(words(out_1)[:, half(h)], y_codes[:, half(h)])
         for q in range(4):
             eng = nc.scalar if q % 2 == 0 else nc.sync
             eng.dma_start(out_2[0, 4 * q : 4 * q + 4, :].bitcast(I32), y_scales[32 * q : 32 * q + 4, :].bitcast(I32))

from contextlib import ExitStack

import concourse.mybir as mybir

K, T, J, R, F, N, Z = 512, 512, 256, 512, 512, 512, 512
FLOPS = 2 * J * (K * R + F * R + R * N)

F32 = mybir.dt.float32
BF16 = mybir.dt.bfloat16
I32 = mybir.dt.int32
U16 = mybir.dt.uint16
U8 = mybir.dt.uint8
E4M3 = mybir.dt.float8_e4m3fn_x4
E5M2 = mybir.dt.float8_e5m2_x4
ALU = mybir.AluOpType
COPY = mybir.ActivationFunctionType.Copy

P = 128
PACK = 4
HALVES = 2
JH = J // HALVES
RUN = 4
STEP_FACTOR = 0.6


def tile_list_two_offsetpicks_own_stepgap_timeslook_pl_kernel(
    tc, xf, ow, fk, w_words, w_scales, sx_words, sx_scales, w2_words, w2_scales, wb_words, wb_scales, tz, offs, offs2,
    out_0, out_1, out_2,
):
    nc = tc.nc
    with ExitStack() as ctx:
        sb = ctx.enter_context(tc.tile_pool(name="sb", bufs=1))
        staging = ctx.enter_context(tc.tile_pool(name="staging", bufs=1))
        psum = ctx.enter_context(tc.psum_pool(name="psum", bufs=1))

        def tile(shape, dtype, name):
            return sb.tile(shape, dtype, name=name, align_bytes=64)

        def planes(x):
            return x.rearrange("(p t) c -> p t c", t=PACK)

        def words(x):
            return x[0].rearrange("p c t -> p (c t)").bitcast(I32)

        def half(h):
            return slice(h * JH, (h + 1) * JH)

        offsets = sb.tile([P, J // 16], U16, name="offsets")
        offsets2 = sb.tile([P, J // 16], U16, name="offsets2")
        def shared(shape, dtype, name, tag):
            return sb.tile(shape, dtype, name=name, tag=tag, align_bytes=64)

        xf_a = shared([P, 2, T], F32, "xf_a", "table_a")
        xf_b = shared([P, T], F32, "xf_b", "table_b")
        xf_c = shared([P, T], F32, "xf_c", "table_c")
        ow_sb = tile([P, PACK, J], F32, "ow_sb")
        fk_sb = tile([P, PACK], F32, "fk_sb")
        W2, W, WB = 0, 1, 2
        raw_scales = staging.tile([P, 3 * R], U8, name="raw_scales", offset=4 * R - 3 * R // 2, align_bytes=64)
        raw_w2 = tile([P, R], I32, "raw_w2")
        dealt = [shared([P, R], I32, "dealt_w2", "picked"), tile([P, R], I32, "dealt_w"), None]
        sx_sb = tile([P, J], I32, "sx_sb")
        scales = tile([P, 3 * R + J], U8, "scales")

        def load_scales(dst, src):
            nc.sync.dma_start(dst.bitcast(I32), src[0].bitcast(I32).partition_broadcast(P // 16))

        q_sb = tile([P, (J + 1) * PACK], F32, "q_sb")
        zero = tile([P, PACK], F32, "zero")
        nc.vector.memset(zero[:], 0.0)
        nc.scalar.activation(q_sb[:, 0:PACK], zero[:], COPY)

        for i, src in ((W2, w2_scales), (W, w_scales), (WB, wb_scales)):
            load_scales(raw_scales[:, i * R : (i + 1) * R], src)
        load_scales(scales[:, 3 * R :], sx_scales)
        nc.sync.dma_start(offsets[:], offs)
        nc.sync.dma_start(xf_a[:], planes(xf)[:, 0:2, :])
        nc.sync.dma_start(fk_sb[:], fk.rearrange("(p t) o -> p (t o)", t=PACK))
        nc.sync.dma_start(ow_sb[:], planes(ow))
        nc.sync.dma_start(offsets2[:], offs2)
        nc.sync.dma_start(xf_b[:], planes(xf)[:, 2, :])
        nc.sync.dma_start(xf_c[:], planes(xf)[:, 3, :])
        nc.sync.dma_start(raw_w2[:], words(w2_words))
        nc.sync.dma_start(sx_sb[:], words(sx_words))

        nc.vector.tensor_copy(
            scales[:, 0 : 3 * R].rearrange("p (w t m) -> p t w m", w=3, t=PACK),
            raw_scales[:].rearrange("p (w m t) -> p t w m", w=3, t=PACK),
        )
        for q in range(1, 4):
            nc.sync.dma_start(scales[32 * q : 32 * q + 4, :].bitcast(I32), scales[4 * q : 4 * q + 4, :].bitcast(I32))

        raw_w = staging.tile([P, R], I32, name="raw_w", offset=0, align_bytes=64)
        raw_wb = staging.tile([P, R], I32, name="raw_wb", offset=4 * R, align_bytes=64)
        raw = [raw_w2, raw_w, raw_wb]
        nc.sync.dma_start(raw_w[:], words(w_words))
        nc.sync.dma_start(raw_wb[:], words(wb_words))

        def deal(i):
            nc.vector.tensor_copy(
                dealt[i][:].rearrange("p (t c i) -> p c t i", t=PACK, i=RUN),
                raw[i][:].rearrange("p (c i t) -> p c t i", t=PACK, i=RUN),
            )

        def product(acc, i, fmt, rhs, rhs_scale):
            for t in range(PACK):
                nc.tensor.matmul_mx(
                    out=acc[:, t, :],
                    lhsT=dealt[i][:, t * P : (t + 1) * P].bitcast(fmt),
                    lhsT_scale=scales[:, i * R + t * P : i * R + (t + 1) * P],
                    rhs=rhs,
                    rhs_scale=rhs_scale,
                    start=True,
                    stop=True,
                )

        def woven(x):
            return x.rearrange("p (c i t) -> p c t i", t=PACK, i=RUN)

        def by_plane(x):
            return x.rearrange("p t (c i) -> p c t i", i=RUN)

        xg = tile([P, 2, J], F32, "xg")
        diff = tile([P, PACK, J], F32, "diff")
        u_pl = shared([P, PACK, J], BF16, "u_pl", "late_weight")

        def scale(t):
            nc.scalar.activation(u_pl[:, t, :], diff[:, t, :], COPY, scale=fk_sb[:, t : t + 1])

        for t in range(2):
            nc.scalar.activation(xg[:, t, :], xf_a[:, t, :].indirect(offsets[:]), COPY)
        for t in range(2):
            nc.vector.tensor_tensor(diff[:, t, :], xg[:, t, :], ow_sb[:, t, :], ALU.subtract)
            scale(t)
        for t, win in ((2, xf_b), (3, xf_c)):
            nc.vector.tensor_tensor(diff[:, t, :], win[:].indirect(offsets[:]), ow_sb[:, t, :], ALU.subtract)
            scale(t)

        tz_a = shared([P, 2, Z], F32, "tz_a", "table_a")
        tz_b = shared([P, Z], F32, "tz_b", "table_b")
        tz_c = shared([P, Z], F32, "tz_c", "table_c")
        tz_win = [tz_a[:, 0, :], tz_a[:, 1, :], tz_b[:], tz_c[:]]
        nc.sync.dma_start(tz_a[:], planes(tz)[:, 0:2, :])
        nc.sync.dma_start(tz_b[:], planes(tz)[:, 2, :])
        nc.sync.dma_start(tz_c[:], planes(tz)[:, 3, :])

        deal(W2)
        q_ps = [psum.tile([P, PACK, JH], F32, name=f"q_ps{h}") for h in range(HALVES)]
        for h in range(HALVES):
            product(q_ps[h], W2, E5M2, sx_sb[:, half(h)].bitcast(E4M3), scales[:, 3 * R + h * JH : 3 * R + (h + 1) * JH])

        u_bf = [tile([P, JH * PACK], BF16, f"u_bf{h}") for h in range(HALVES)]
        u_codes = [tile([P, JH], I32, f"u_codes{h}") for h in range(HALVES)]
        u_scales = [tile([P, JH], U8, f"u_scales{h}") for h in range(HALVES)]
        nc.vector.tensor_copy(woven(u_bf[0][:]), by_plane(u_pl[:, :, half(0)]))
        nc.scalar.copy(woven(u_bf[1][:]), by_plane(u_pl[:, :, half(1)]))
        deal(W)
        a_ps = [psum.tile([P, PACK, JH], F32, name=f"a_ps{h}") for h in range(HALVES)]
        p_ps = [psum.tile([P, PACK, JH], F32, name=f"p_ps{h}") for h in range(HALVES)]
        step = tile([P, J * PACK], F32, "step")
        hid_bf = [tile([P, JH * PACK], BF16, f"hid_bf{h}") for h in range(HALVES)]
        hid_codes = [tile([P, JH], I32, f"hid_codes{h}") for h in range(HALVES)]
        hid_scales = [tile([P, JH], U8, f"hid_scales{h}") for h in range(HALVES)]

        def first(h):
            nc.vector.quantize_mx(out=u_codes[h][:].bitcast(E5M2), scales=u_scales[h][:], in_=u_bf[h][:])
            product(a_ps[h], W, E5M2, u_codes[h][:].bitcast(E5M2), u_scales[h][:])

        def stepped(h):
            lo, hi = h * JH * PACK, (h + 1) * JH * PACK
            nc.scalar.activation(
                q_sb[:, lo + PACK : hi + PACK].rearrange("p (j t) -> p j t", t=PACK),
                q_ps[h][:].rearrange("p t j -> p j t"),
                COPY,
            )
            nc.vector.scalar_tensor_tensor(
                step[:, lo:hi], q_sb[:, lo:hi], -STEP_FACTOR, q_sb[:, lo + PACK : hi + PACK], ALU.mult, ALU.add
            )

        def hidden(h):
            nc.vector.tensor_tensor(
                hid_bf[h][:].rearrange("p (j t) -> p j t", t=PACK),
                a_ps[h][:].rearrange("p t j -> p j t"),
                step[:, h * JH * PACK : (h + 1) * JH * PACK].rearrange("p (j t) -> p j t", t=PACK),
                ALU.max,
            )

        def second(h):
            nc.vector.quantize_mx(out=hid_codes[h][:].bitcast(E5M2), scales=hid_scales[h][:], in_=hid_bf[h][:])
            product(p_ps[h], WB, E4M3, hid_codes[h][:].bitcast(E5M2), hid_scales[h][:])

        first(0)
        dealt[WB] = shared([P, R], I32, "dealt_wb", "late_weight")
        deal(WB)
        stepped(0)
        first(1)
        hidden(0)
        stepped(1)
        second(0)
        hidden(1)
        second(1)

        tzg = shared([P, PACK, J], F32, "tzg", "picked")
        for t in range(PACK):
            nc.scalar.activation(tzg[:, t, :], tz_win[t].indirect(offsets2[:]), COPY)

        y = [tile([P, PACK, JH], F32, f"y{h}") for h in range(HALVES)]
        y_bf = [tile([P, JH * PACK], BF16, f"y_bf{h}") for h in range(HALVES)]
        y_codes = tile([P, J], I32, "y_codes")
        y_scales = tile([P, J], U8, "y_scales")
        for h in range(HALVES):
            nc.vector.tensor_tensor(y[h][:], p_ps[h][:], tzg[:, :, half(h)], ALU.mult)
            nc.sync.dma_start(planes(out_0)[:, :, half(h)], y[h][:])
        nc.scalar.activation(woven(y_bf[0][:]), by_plane(y[0][:]), COPY)
        nc.vector.tensor_copy(woven(y_bf[1][:]), by_plane(y[1][:]))
        for h in range(HALVES):
            nc.vector.quantize_mx(out=y_codes[:, half(h)].bitcast(E4M3), scales=y_scales[:, half(h)], in_=y_bf[h][:])
            nc.sync.dma_start(words(out_1)[:, half(h)], y_codes[:, half(h)])
        for q in range(4):
            eng = nc.scalar if q % 2 == 0 else nc.sync
            eng.dma_start(out_2[0, 4 * q : 4 * q + 4, :].bitcast(I32), y_scales[32 * q : 32 * q + 4, :].bitcast(I32))
